import numpy as np
import ml_dtypes


def mxq(x, axis, fmt="e4m3"):
    dtype, down = {"e4m3": (ml_dtypes.float8_e4m3fn, 7), "e5m2": (ml_dtypes.float8_e5m2, 14)}[fmt]
    v = np.moveaxis(np.asarray(x, np.float32).astype(ml_dtypes.bfloat16).astype(np.float64), axis, -1)
    blocks = v.reshape(v.shape[:-1] + (-1, 32))
    amax = np.abs(blocks).max(-1, keepdims=True)
    byte = np.maximum(np.where(amax > 0, np.frexp(amax)[1] - 1 + 127, 0) - down, 1)
    scale = np.exp2(byte - 127.0)
    codes = (blocks / scale).astype(np.float32).astype(dtype).astype(np.float64)
    return np.moveaxis((codes * scale).reshape(v.shape), -1, axis)


WIDE = False


def mx_kscale(k):
    if not WIDE:
        return np.ones(k)
    levels = np.array([10, -10, 5, -5, 0])
    if k % 512:
        return np.exp2(np.random.permutation(np.resize(levels, k // 32))).repeat(32)
    a = np.empty((k // 512, 16))
    for p in range(k // 512):
        a[p, :8] = np.random.permutation(np.resize(levels, 8))
        for g in range(8):
            far = levels[np.abs(levels - a[p, g]) >= 10]
            a[p, g + 8] = far[np.random.randint(len(far))]
    return np.exp2(a.ravel()).repeat(32)


def f64(x):
    return np.asarray(x).astype(np.float64)


def striped(idx):
    return np.tile(idx.reshape(-1, 16).T, (8, 1)).astype(np.uint16)


def unstriped(offs):
    return offs[:16].T.reshape(-1).astype(np.int64)


def striped8(idx):
    return np.concatenate([x.reshape(-1, 16).T for x in idx]).astype(np.uint16)


def runs(offs, k):
    lists = np.stack([offs[16 * r : 16 * r + 16].T.reshape(-1) for r in range(8)]).astype(np.int64)
    return lists[np.arange(k) % 512 // 64]


def pack_weight(w):
    k, n = w.shape
    w = f64(np.asarray(w, np.float32).astype(ml_dtypes.bfloat16)).reshape(k // 32, 32, n)
    amax = np.abs(w).max(1)
    byte = np.clip(np.where(amax > 0, np.frexp(amax)[1] - 1 + 127 - 7, 1), 1, 254)
    scaled = (w * np.exp2(127.0 - byte)[:, None, :]).reshape(k, n).astype(np.float32)
    words = np.ascontiguousarray(scaled.reshape(k // 512, 128, 4, n).transpose(0, 1, 3, 2)).astype(ml_dtypes.float8_e4m3fn).view(np.uint8)
    return words, np.ascontiguousarray(byte.astype(np.uint8).reshape(k // 512, 16, n))


def unpack_weight(words, scales):
    g, p, n, _ = words.shape
    vals = np.ascontiguousarray(words).view(ml_dtypes.float8_e4m3fn).astype(np.float64) * np.repeat(np.exp2(scales.astype(np.float64) - 127.0), 8, axis=1)[..., None]
    return vals.transpose(0, 1, 3, 2).reshape(g * 512, n)


def sigmoid(v):
    return 1.0 / (1.0 + np.exp(-np.maximum(v, -700.0)))

def planes(y):
    n, m = y.shape
    v = y.astype(np.float32).astype(ml_dtypes.bfloat16).astype(np.float64).reshape(n // 32, 32, m)
    top = np.abs(v).max(1)
    byte = np.clip(np.where(top > 0, np.frexp(top)[1] - 1 + 127 - 7, 1), 1, 254)
    codes = (v * np.exp2(127.0 - byte)[:, None, :]).reshape(n, m).astype(np.float32).astype(ml_dtypes.float8_e4m3fn).view(np.uint8)
    words = codes.reshape(n // 512, 128, 4, m).transpose(0, 1, 3, 2)
    return np.ascontiguousarray(words), np.ascontiguousarray(byte.astype(np.uint8).reshape(n // 512, 16, m))


K, T, S, G, H, W = 512, 2048, 512, 2048, 512, 384


def setup_inputs():
    n = np.random.standard_normal
    s = mx_kscale(K)[:, None]
    packed_xT = pack_weight(n((K, T)) * s)
    packed_dT = pack_weight(n((K, G)) / s)
    return {
        "x_words": packed_xT[0],
        "x_scales": packed_xT[1],
        "d_words": packed_dT[0],
        "d_scales": packed_dT[1],
        "gs": (np.random.uniform(0.5, 1.5, (K, 1)) * s).astype(np.float32),
        "offs": striped(np.random.permutation(T)[:S]),
        "k1": striped8(np.random.randint(0, G, (8, H))),
        "n1": striped(np.random.permutation(S)),
        "n2": striped(np.random.permutation(S)),
        "n3": striped(np.random.permutation(S)[:W]),
        "n4": striped(np.random.permutation(S)[:W]),
    }


def reference(x_words, x_scales, d_words, d_scales, gs, offs, k1, n1, n2, n3, n4):
    d_k1 = unpack_weight(d_words, d_scales)[np.arange(K)[:, None], runs(k1, K)]
    xq = unpack_weight(x_words, x_scales)[:, unstriped(offs)]
    h = 0.0625 * (d_k1.T @ xq)
    st = h[:, unstriped(n1)] - h
    z = f64(gs) * (h * (sigmoid(st[:, unstriped(n2)])))
    h2 = 0.0625 * ((d_k1.T @ mxq(z, 0, "e4m3")))
    old = h2[:, unstriped(n3)]
    pa = h2[:, unstriped(n4)]
    ra = old - np.tanh(pa)
    out = h2.copy()
    out[:, unstriped(n3)] = ra
    return (out,) + planes(out)

@@ -1,0 +1,198 @@
+import concourse.mybir as mybir
+
+F32 = mybir.dt.float32
+BF16 = mybir.dt.bfloat16
+I32 = mybir.dt.int32
+U32 = mybir.dt.uint32
+U16 = mybir.dt.uint16
+U8 = mybir.dt.uint8
+FP8X4 = mybir.dt.float8_e4m3fn_x4
+ACT = mybir.ActivationFunctionType
+ALU = mybir.AluOpType
+
+P = 128
+PACK = 4
+TABLE = 2048
+S = 512
+W = 384
+SPARE = 16
+SIXTEENTH = 0.0625
+PIECES = ((0, 128), (128, 256), (384, 128))
+
+FLOPS = 2 * 2 * 512 * 512 * 512
+
+
+def tile_picked_ringhopdktanh_none_po_kernel(
+    tc, x_words, x_scales, d_words, d_scales, gs, offs, k1, n1, n2, n3, n4, out_0, out_1, out_2
+):
+    nc = tc.nc
+    with (
+        tc.tile_pool(name="keep", bufs=1) as keep,
+        tc.psum_pool(name="psum", bufs=1) as psum,
+    ):
+
+        def sb(name, shape, dtype):
+            return keep.tile(shape, dtype, name=name, align_bytes=64)
+
+        def entries(lst, start, count):
+            return lst[:, start // 16 : (start + count) // 16]
+
+        k1_sb = sb("k1_sb", [P, S // 16], U16)
+        offs_sb = sb("offs_sb", [P, S // 16], U16)
+        n1_sb = sb("n1_sb", [P, S // 16], U16)
+        n2_sb = sb("n2_sb", [P, S // 16], U16)
+        n3_sb = sb("n3_sb", [P, W // 16], U16)
+        n4_sb = sb("n4_sb", [P, W // 16], U16)
+        d_table = sb("d_table", [P, TABLE], U32)
+        x_table = sb("x_table", [P, TABLE], U32)
+        d_table_sc = sb("d_table_sc", [P, TABLE], U8)
+        x_table_sc = sb("x_table_sc", [P, TABLE], U8)
+        d_sc = sb("d_sc", [P, S], U8)
+        sc_placed = sb("sc_placed", [P, 2 * S], U8)
+        gs_sb = sb("gs_sb", [P, PACK], F32)
+        h = [sb("h%d" % t, [P, S + SPARE], F32) for t in range(PACK)]
+
+        nc.gpsimd.memset(sc_placed[:].bitcast(I32), 0)
+        for t in range(PACK):
+            nc.gpsimd.memset(h[t][:, S:], 0.0)
+
+        def load_scales(tile, rows):
+            nc.sync.dma_start(tile[:].bitcast(I32), rows[0].bitcast(I32).unsqueeze(1).broadcast_to([16, 8, TABLE // 4]))
+
+        def load_words(tile, words):
+            nc.sync.dma_start(tile[:].bitcast(I32), words[0].rearrange("p n t -> p (n t)").bitcast(I32))
+
+        nc.sync.dma_start(k1_sb[:], k1)
+        load_scales(d_table_sc, d_scales)
+        nc.sync.dma_start(offs_sb[:], offs)
+        load_scales(x_table_sc, x_scales)
+        nc.sync.dma_start(gs_sb[:], gs.rearrange("(p t) o -> p (t o)", t=PACK))
+        nc.sync.dma_start(n1_sb[:], n1)
+        nc.sync.dma_start(n2_sb[:], n2)
+        load_words(d_table, d_words)
+        load_words(x_table, x_words)
+        nc.sync.dma_start(n3_sb[:], n3)
+        nc.sync.dma_start(n4_sb[:], n4)
+
+        sc_picked = sb("sc_picked", [P, 2 * S], U8)
+        nc.vector.tensor_copy(sc_picked[:, :S], d_table_sc[:].indirect(k1_sb[:]))
+        nc.vector.tensor_copy(sc_picked[:, S:], x_table_sc[:].indirect(offs_sb[:]))
+        for r in range(4):
+            nc.sync.dma_start(sc_placed[r:P:32, :].bitcast(I32), sc_picked[8 * r : P : 32, :].bitcast(I32))
+        x_sc = sc_placed[:, S:]
+
+        d_picked = sb("d_picked", [P, S], U32)
+        d_codes = sb("d_codes", [P, S], U32)
+        nc.vector.tensor_copy(d_picked[:], d_table[:].indirect(k1_sb[:]))
+        nc.vector.tensor_copy(
+            d_codes[:].bitcast(I32).rearrange("p (t m) -> p m t", t=PACK),
+            d_picked[:].bitcast(I32).rearrange("p (m t) -> p m t", t=PACK),
+        )
+        nc.vector.tensor_copy(
+            d_sc[:].rearrange("p (t m) -> p m t", t=PACK), sc_placed[:, :S].rearrange("p (m t) -> p m t", t=PACK)
+        )
+        x_codes = sb("x_codes", [P, S], U32)
+        nc.vector.tensor_copy(x_codes[:], x_table[:].indirect(offs_sb[:]))
+
+        gs16 = sb("gs16", [P, PACK], F32)
+        nc.scalar.activation(gs16[:], gs_sb[:], ACT.Copy, scale=SIXTEENTH)
+
+        def product(acc, t, codes, scales):
+            cols = slice(t * P, (t + 1) * P)
+            nc.tensor.matmul_mx(
+                out=acc,
+                lhsT=d_codes[:, cols].bitcast(FP8X4),
+                lhsT_scale=d_sc[:, cols],
+                rhs=codes.bitcast(FP8X4),
+                rhs_scale=scales,
+                start=True,
+                stop=True,
+            )
+
+        acc1 = [psum.tile([P, S], F32, name="acc1_%d" % t) for t in range(PACK)]
+        hop = [sb("hop%d" % t, [P, S], F32) for t in range(PACK)]
+        st = [sb("st%d" % t, [P, S], F32) for t in range(PACK)]
+        for t in range(PACK):
+            product(acc1[t][:], t, x_codes[:], x_sc)
+            nc.vector.tensor_scalar(h[t][:, :S], acc1[t][:], SIXTEENTH, None, ALU.mult)
+        for t in range(PACK):
+            nc.scalar.activation(hop[t][:], h[t][:].indirect(n1_sb[:]), ACT.Copy)
+            nc.vector.scalar_tensor_tensor(st[t][:], acc1[t][:], -SIXTEENTH, hop[t][:], ALU.mult, ALU.add)
+
+        first = psum.tile([P, PACK, 128], F32, name="first")
+        middle = [psum.tile([P, 2, 256], F32, name="middle%d" % u) for u in range(2)]
+        acc2 = [
+            [first[:, t, :] for t in range(PACK)],
+            [middle[t // 2][:, t % 2, :] for t in range(PACK)],
+            [acc1[t][:, :128] for t in range(PACK)],
+        ]
+        h2 = [sb("h2_%d" % t, [P, S], F32) for t in range(PACK)]
+        gate = [sb("gate%d" % t, [P, 256], F32) for t in range(PACK)]
+        for i, (start, width) in enumerate(PIECES):
+            z_rows = sb("z_rows%d" % i, [P, PACK, width], BF16)
+            z_words = sb("z_words%d" % i, [P, width, PACK], BF16)
+            z_codes = sb("z_codes%d" % i, [P, width], U32)
+            z_sc = sb("z_sc%d" % i, [P, width], U8)
+            for t in range(PACK):
+                nc.scalar.activation(gate[t][:, :width], st[t][:].indirect(entries(n2_sb, start, width)), ACT.Sigmoid)
+                nc.vector.scalar_tensor_tensor(
+                    z_rows[:, t, :], acc1[t][:, start : start + width], gs16[:, t : t + 1], gate[t][:, :width], ALU.mult, ALU.mult
+                )
+            nc.vector.tensor_copy(
+                z_words[:].rearrange("p (c i) t -> p c t i", i=4), z_rows[:].rearrange("p t (c i) -> p c t i", i=4)
+            )
+            nc.vector.quantize_mx(
+                out=z_codes[:].bitcast(FP8X4), scales=z_sc[:], in_=z_words[:].rearrange("p c t -> p (c t)")
+            )
+            for t in range(PACK):
+                product(acc2[i][t], t, z_codes[:], z_sc[:])
+
+        y_words = [sb("y_words%d" % u, [P, S // 2, PACK], BF16) for u in range(2)]
+        y_codes = sb("y_codes", [P, S], U32)
+        y_sc = sb("y_sc", [P, S], U8)
+        out_rows = out_0.rearrange("(p t) c -> t p c", t=PACK)
+        old = [sb("old%d" % t, [P, W], F32) for t in range(PACK)]
+        neg_tanh = [sb("neg_tanh%d" % t, [P, S], F32) for t in range(PACK)]
+        ra = [sb("ra%d" % t, [P, W], F32) for t in range(PACK)]
+        y = [sb("y%d" % t, [P, S], F32) for t in range(PACK)]
+
+        def cols_of(i):
+            start, width = PIECES[i]
+            return slice(start, start + width)
+
+        last = len(PIECES) - 1
+        for i in range(last):
+            nc.scalar.activation(h2[0][:, cols_of(i)], acc2[i][0], ACT.Copy, scale=SIXTEENTH)
+            for t in range(PACK):
+                nc.scalar.activation(neg_tanh[t][:, cols_of(i)], acc2[i][t], ACT.Tanh, scale=-SIXTEENTH)
+
+        nc.scalar.activation(h2[0][:, cols_of(last)], acc2[last][0], ACT.Copy, scale=SIXTEENTH)
+        for t in range(1, PACK):
+            for i in range(len(PIECES)):
+                nc.vector.tensor_scalar(h2[t][:, cols_of(i)], acc2[i][t], SIXTEENTH, None, ALU.mult)
+        for t in range(PACK):
+            nc.scalar.activation(old[t][:], h2[t][:].indirect(n3_sb[:]), ACT.Copy)
+            nc.scalar.activation(neg_tanh[t][:, cols_of(last)], acc2[last][t], ACT.Tanh, scale=-SIXTEENTH)
+        for t in range(PACK):
+            nc.vector.tensor_copy(y[t][:], h2[t][:])
+            nc.vector.tensor_tensor(ra[t][:], neg_tanh[t][:].indirect(n4_sb[:]), old[t][:], ALU.add)
+
+        def put(t):
+            nc.scalar.activation(y[t][:].indirect(n3_sb[:]), ra[t][:], ACT.Copy)
+            nc.sync.dma_start(out_rows[t], y[t][:])
+            for u in range(2):
+                nc.vector.tensor_copy(y_words[u][:, :, t], y[t][:, u * S // 2 : (u + 1) * S // 2])
+
+        for t in range(PACK):
+            put(t)
+
+        out_words = out_1[0].rearrange("p n t -> p (n t)").bitcast(I32)
+        for u in range(2):
+            cols = slice(u * S // 2, (u + 1) * S // 2)
+            nc.vector.quantize_mx(
+                out=y_codes[:, cols].bitcast(FP8X4), scales=y_sc[:, cols], in_=y_words[u][:].rearrange("p c t -> p (c t)")
+            )
+            nc.sync.dma_start(out_words[:, cols], y_codes[:, cols].bitcast(I32))
+        for q in range(4):
+            queue = nc.scalar if q % 2 == 0 else nc.sync
+            queue.dma_start(out_2[0, 4 * q : 4 * q + 4, :].bitcast(I32), y_sc[32 * q : 32 * q + 4, :].bitcast(I32))

@@ -94,6 +94,8 @@ def tile_picked_ringhopdktanh_none_po_kernel(
         x_codes = sb("x_codes", [P, S], U32)
         nc.vector.tensor_copy(x_codes[:], x_table[:].indirect(offs_sb[:]))
 
+        warm = sb("warm", [P, 1], F32)
+        nc.scalar.activation(warm[:], gs_sb[:, 0:1], ACT.Sigmoid)
         gs16 = sb("gs16", [P, PACK], F32)
         nc.scalar.activation(gs16[:], gs_sb[:], ACT.Copy, scale=SIXTEENTH)
 

@@ -17,7 +17,9 @@ S = 512
 W = 384
 SPARE = 16
 SIXTEENTH = 0.0625
-PIECES = ((0, 128), (128, 256), (384, 128))
+PIECES = ((0, 256), (256, 128), (384, 128))
+
+EARLY = 384
 
 FLOPS = 2 * 2 * 512 * 512 * 512
 
@@ -47,7 +49,6 @@ def tile_picked_ringhopdktanh_none_po_kernel(
         x_table = sb("x_table", [P, TABLE], U32)
         d_table_sc = sb("d_table_sc", [P, TABLE], U8)
         x_table_sc = sb("x_table_sc", [P, TABLE], U8)
-        d_sc = sb("d_sc", [P, S], U8)
         sc_placed = sb("sc_placed", [P, 2 * S], U8)
         gs_sb = sb("gs_sb", [P, PACK], F32)
         h = [sb("h%d" % t, [P, S + SPARE], F32) for t in range(PACK)]
@@ -74,11 +75,18 @@ def tile_picked_ringhopdktanh_none_po_kernel(
         nc.sync.dma_start(n3_sb[:], n3)
         nc.sync.dma_start(n4_sb[:], n4)
 
-        sc_picked = sb("sc_picked", [P, 2 * S], U8)
-        nc.vector.tensor_copy(sc_picked[:, :S], d_table_sc[:].indirect(k1_sb[:]))
-        nc.vector.tensor_copy(sc_picked[:, S:], x_table_sc[:].indirect(offs_sb[:]))
+        d_sc_picked = sb("d_sc_picked", [P, S], U8)
+        x_sc_picked = sb("x_sc_picked", [P, S], U8)
+        sc_joined = sb("sc_joined", [P, 2 * S], U8)
+        nc.vector.tensor_copy(d_sc_picked[:], d_table_sc[:].indirect(k1_sb[:]))
+        nc.vector.tensor_copy(
+            sc_joined[:, :S].rearrange("p (t m) -> p m t", t=PACK), d_sc_picked[:].rearrange("p (m t) -> p m t", t=PACK)
+        )
+        nc.vector.tensor_copy(x_sc_picked[:], x_table_sc[:].indirect(offs_sb[:]))
+        nc.vector.tensor_copy(sc_joined[:, S:].bitcast(I32), x_sc_picked[:].bitcast(I32))
         for r in range(4):
-            nc.sync.dma_start(sc_placed[r:P:32, :].bitcast(I32), sc_picked[8 * r : P : 32, :].bitcast(I32))
+            nc.sync.dma_start(sc_placed[r:P:32, :].bitcast(I32), sc_joined[8 * r : P : 32, :].bitcast(I32))
+        d_sc = sc_placed[:, :S]
         x_sc = sc_placed[:, S:]
 
         d_picked = sb("d_picked", [P, S], U32)
@@ -88,11 +96,9 @@ def tile_picked_ringhopdktanh_none_po_kernel(
             d_codes[:].bitcast(I32).rearrange("p (t m) -> p m t", t=PACK),
             d_picked[:].bitcast(I32).rearrange("p (m t) -> p m t", t=PACK),
         )
-        nc.vector.tensor_copy(
-            d_sc[:].rearrange("p (t m) -> p m t", t=PACK), sc_placed[:, :S].rearrange("p (m t) -> p m t", t=PACK)
-        )
         x_codes = sb("x_codes", [P, S], U32)
-        nc.vector.tensor_copy(x_codes[:], x_table[:].indirect(offs_sb[:]))
+        for start, width in ((0, EARLY), (EARLY, S - EARLY)):
+            nc.vector.tensor_copy(x_codes[:, start : start + width], x_table[:].indirect(entries(offs_sb, start, width)))
 
         warm = sb("warm", [P, 1], F32)
         nc.scalar.activation(warm[:], gs_sb[:, 0:1], ACT.Sigmoid)
@@ -114,18 +120,34 @@ def tile_picked_ringhopdktanh_none_po_kernel(
         acc1 = [psum.tile([P, S], F32, name="acc1_%d" % t) for t in range(PACK)]
         hop = [sb("hop%d" % t, [P, S], F32) for t in range(PACK)]
         st = [sb("st%d" % t, [P, S], F32) for t in range(PACK)]
-        for t in range(PACK):
+        late0 = psum.tile([P, S - EARLY], F32, name="late0")
+
+        def sums1(t, start, width):
+            if t == 0 and start >= EARLY:
+                return late0[:, start - EARLY : start - EARLY + width]
+            return acc1[t][:, start : start + width]
+
+        for start, width in ((0, 256), (256, 128), (EARLY, S - EARLY)):
+            cols = slice(start, start + width)
+            product(sums1(0, start, width), 0, x_codes[:, cols], x_sc[:, cols])
+        for start, width in ((0, EARLY), (EARLY, S - EARLY)):
+            nc.scalar.activation(h[0][:, start : start + width], sums1(0, start, width), ACT.Copy, scale=SIXTEENTH)
+        for t in range(1, PACK):
             product(acc1[t][:], t, x_codes[:], x_sc)
             nc.vector.tensor_scalar(h[t][:, :S], acc1[t][:], SIXTEENTH, None, ALU.mult)
         for t in range(PACK):
             nc.scalar.activation(hop[t][:], h[t][:].indirect(n1_sb[:]), ACT.Copy)
-            nc.vector.scalar_tensor_tensor(st[t][:], acc1[t][:], -SIXTEENTH, hop[t][:], ALU.mult, ALU.add)
+            for start, width in ((0, EARLY), (EARLY, S - EARLY)) if t == 0 else ((0, S),):
+                cols = slice(start, start + width)
+                nc.vector.scalar_tensor_tensor(
+                    st[t][:, cols], sums1(t, start, width), -SIXTEENTH, hop[t][:, cols], ALU.mult, ALU.add
+                )
 
         first = psum.tile([P, PACK, 128], F32, name="first")
         middle = [psum.tile([P, 2, 256], F32, name="middle%d" % u) for u in range(2)]
         acc2 = [
-            [first[:, t, :] for t in range(PACK)],
             [middle[t // 2][:, t % 2, :] for t in range(PACK)],
+            [first[:, t, :] for t in range(PACK)],
             [acc1[t][:, :128] for t in range(PACK)],
         ]
         h2 = [sb("h2_%d" % t, [P, S], F32) for t in range(PACK)]
@@ -138,7 +160,7 @@ def tile_picked_ringhopdktanh_none_po_kernel(
             for t in range(PACK):
                 nc.scalar.activation(gate[t][:, :width], st[t][:].indirect(entries(n2_sb, start, width)), ACT.Sigmoid)
                 nc.vector.scalar_tensor_tensor(
-                    z_rows[:, t, :], acc1[t][:, start : start + width], gs16[:, t : t + 1], gate[t][:, :width], ALU.mult, ALU.mult
+                    z_rows[:, t, :], sums1(t, start, width), gs16[:, t : t + 1], gate[t][:, :width], ALU.mult, ALU.mult
                 )
             nc.vector.tensor_copy(
                 z_words[:].rearrange("p (c i) t -> p c t i", i=4), z_rows[:].rearrange("p t (c i) -> p c t i", i=4)

@@ -53,6 +53,7 @@ def tile_picked_ringhopdktanh_none_po_kernel(
         gs_sb = sb("gs_sb", [P, PACK], F32)
         h = [sb("h%d" % t, [P, S + SPARE], F32) for t in range(PACK)]
 
+        nc.gpsimd.memset(x_table_sc[:].bitcast(I32), 0)
         nc.gpsimd.memset(sc_placed[:].bitcast(I32), 0)
         for t in range(PACK):
             nc.gpsimd.memset(h[t][:, S:], 0.0)
@@ -66,7 +67,7 @@ def tile_picked_ringhopdktanh_none_po_kernel(
         nc.sync.dma_start(k1_sb[:], k1)
         load_scales(d_table_sc, d_scales)
         nc.sync.dma_start(offs_sb[:], offs)
-        load_scales(x_table_sc, x_scales)
+        nc.scalar.dma_start(x_table_sc[0:P:8, :].bitcast(I32), x_scales[0].bitcast(I32))
         nc.sync.dma_start(gs_sb[:], gs.rearrange("(p t) o -> p (t o)", t=PACK))
         nc.sync.dma_start(n1_sb[:], n1)
         nc.sync.dma_start(n2_sb[:], n2)

import concourse.mybir as mybir

F32 = mybir.dt.float32
BF16 = mybir.dt.bfloat16
I32 = mybir.dt.int32
U32 = mybir.dt.uint32
U16 = mybir.dt.uint16
U8 = mybir.dt.uint8
FP8X4 = mybir.dt.float8_e4m3fn_x4
ACT = mybir.ActivationFunctionType
ALU = mybir.AluOpType

P = 128
PACK = 4
TABLE = 2048
S = 512
W = 384
SPARE = 16
SIXTEENTH = 0.0625
PIECES = ((0, 256), (256, 128), (384, 128))

EARLY = 384

FLOPS = 2 * 2 * 512 * 512 * 512


def tile_picked_ringhopdktanh_none_po_kernel(
    tc, x_words, x_scales, d_words, d_scales, gs, offs, k1, n1, n2, n3, n4, out_0, out_1, out_2
):
    nc = tc.nc
    with (
        tc.tile_pool(name="keep", bufs=1) as keep,
        tc.psum_pool(name="psum", bufs=1) as psum,
    ):

        def sb(name, shape, dtype):
            return keep.tile(shape, dtype, name=name, align_bytes=64)

        def entries(lst, start, count):
            return lst[:, start // 16 : (start + count) // 16]

        k1_sb = sb("k1_sb", [P, S // 16], U16)
        offs_sb = sb("offs_sb", [P, S // 16], U16)
        n1_sb = sb("n1_sb", [P, S // 16], U16)
        n2_sb = sb("n2_sb", [P, S // 16], U16)
        n3_sb = sb("n3_sb", [P, W // 16], U16)
        n4_sb = sb("n4_sb", [P, W // 16], U16)
        d_table = sb("d_table", [P, TABLE], U32)
        x_table = sb("x_table", [P, TABLE], U32)
        d_table_sc = sb("d_table_sc", [P, TABLE], U8)
        x_table_sc = sb("x_table_sc", [P, TABLE], U8)
        sc_placed = sb("sc_placed", [P, 2 * S], U8)
        gs_sb = sb("gs_sb", [P, PACK], F32)
        h = [sb("h%d" % t, [P, S + SPARE], F32) for t in range(PACK)]

        nc.gpsimd.memset(x_table_sc[:].bitcast(I32), 0)
        nc.gpsimd.memset(sc_placed[:].bitcast(I32), 0)
        for t in range(PACK):
            nc.gpsimd.memset(h[t][:, S:], 0.0)

        def load_scales(tile, rows):
            nc.sync.dma_start(tile[:].bitcast(I32), rows[0].bitcast(I32).unsqueeze(1).broadcast_to([16, 8, TABLE // 4]))

        def load_words(tile, words):
            nc.sync.dma_start(tile[:].bitcast(I32), words[0].rearrange("p n t -> p (n t)").bitcast(I32))

        nc.sync.dma_start(k1_sb[:], k1)
        load_scales(d_table_sc, d_scales)
        nc.sync.dma_start(offs_sb[:], offs)
        nc.scalar.dma_start(x_table_sc[0:P:8, :].bitcast(I32), x_scales[0].bitcast(I32))
        nc.sync.dma_start(gs_sb[:], gs.rearrange("(p t) o -> p (t o)", t=PACK))
        nc.sync.dma_start(n1_sb[:], n1)
        nc.sync.dma_start(n2_sb[:], n2)
        load_words(d_table, d_words)
        load_words(x_table, x_words)
        nc.sync.dma_start(n3_sb[:], n3)
        nc.sync.dma_start(n4_sb[:], n4)

        d_sc_picked = sb("d_sc_picked", [P, S], U8)
        x_sc_picked = sb("x_sc_picked", [P, S], U8)
        sc_joined = sb("sc_joined", [P, 2 * S], U8)
        nc.vector.tensor_copy(d_sc_picked[:], d_table_sc[:].indirect(k1_sb[:]))
        nc.vector.tensor_copy(
            sc_joined[:, :S].rearrange("p (t m) -> p m t", t=PACK), d_sc_picked[:].rearrange("p (m t) -> p m t", t=PACK)
        )
        nc.vector.tensor_copy(x_sc_picked[:], x_table_sc[:].indirect(offs_sb[:]))
        nc.vector.tensor_copy(sc_joined[:, S:].bitcast(I32), x_sc_picked[:].bitcast(I32))
        for r in range(4):
            nc.sync.dma_start(sc_placed[r:P:32, :].bitcast(I32), sc_joined[8 * r : P : 32, :].bitcast(I32))
        d_sc = sc_placed[:, :S]
        x_sc = sc_placed[:, S:]

        d_picked = sb("d_picked", [P, S], U32)
        d_codes = sb("d_codes", [P, S], U32)
        nc.vector.tensor_copy(d_picked[:], d_table[:].indirect(k1_sb[:]))
        nc.vector.tensor_copy(
            d_codes[:].bitcast(I32).rearrange("p (t m) -> p m t", t=PACK),
            d_picked[:].bitcast(I32).rearrange("p (m t) -> p m t", t=PACK),
        )
        x_codes = sb("x_codes", [P, S], U32)
        for start, width in ((0, EARLY), (EARLY, S - EARLY)):
            nc.vector.tensor_copy(x_codes[:, start : start + width], x_table[:].indirect(entries(offs_sb, start, width)))

        warm = sb("warm", [P, 1], F32)
        nc.scalar.activation(warm[:], gs_sb[:, 0:1], ACT.Sigmoid)
        gs16 = sb("gs16", [P, PACK], F32)
        nc.scalar.activation(gs16[:], gs_sb[:], ACT.Copy, scale=SIXTEENTH)

        def product(acc, t, codes, scales):
            cols = slice(t * P, (t + 1) * P)
            nc.tensor.matmul_mx(
                out=acc,
                lhsT=d_codes[:, cols].bitcast(FP8X4),
                lhsT_scale=d_sc[:, cols],
                rhs=codes.bitcast(FP8X4),
                rhs_scale=scales,
                start=True,
                stop=True,
            )

        acc1 = [psum.tile([P, S], F32, name="acc1_%d" % t) for t in range(PACK)]
        hop = [sb("hop%d" % t, [P, S], F32) for t in range(PACK)]
        st = [sb("st%d" % t, [P, S], F32) for t in range(PACK)]
        late0 = psum.tile([P, S - EARLY], F32, name="late0")

        def sums1(t, start, width):
            if t == 0 and start >= EARLY:
                return late0[:, start - EARLY : start - EARLY + width]
            return acc1[t][:, start : start + width]

        for start, width in ((0, 256), (256, 128), (EARLY, S - EARLY)):
            cols = slice(start, start + width)
            product(sums1(0, start, width), 0, x_codes[:, cols], x_sc[:, cols])
        for start, width in ((0, EARLY), (EARLY, S - EARLY)):
            nc.scalar.activation(h[0][:, start : start + width], sums1(0, start, width), ACT.Copy, scale=SIXTEENTH)
        for t in range(1, PACK):
            product(acc1[t][:], t, x_codes[:], x_sc)
            nc.vector.tensor_scalar(h[t][:, :S], acc1[t][:], SIXTEENTH, None, ALU.mult)
        for t in range(PACK):
            nc.scalar.activation(hop[t][:], h[t][:].indirect(n1_sb[:]), ACT.Copy)
            for start, width in ((0, EARLY), (EARLY, S - EARLY)) if t == 0 else ((0, S),):
                cols = slice(start, start + width)
                nc.vector.scalar_tensor_tensor(
                    st[t][:, cols], sums1(t, start, width), -SIXTEENTH, hop[t][:, cols], ALU.mult, ALU.add
                )

        first = psum.tile([P, PACK, 128], F32, name="first")
        middle = [psum.tile([P, 2, 256], F32, name="middle%d" % u) for u in range(2)]
        acc2 = [
            [middle[t // 2][:, t % 2, :] for t in range(PACK)],
            [first[:, t, :] for t in range(PACK)],
            [acc1[t][:, :128] for t in range(PACK)],
        ]
        h2 = [sb("h2_%d" % t, [P, S], F32) for t in range(PACK)]
        gate = [sb("gate%d" % t, [P, 256], F32) for t in range(PACK)]
        for i, (start, width) in enumerate(PIECES):
            z_rows = sb("z_rows%d" % i, [P, PACK, width], BF16)
            z_words = sb("z_words%d" % i, [P, width, PACK], BF16)
            z_codes = sb("z_codes%d" % i, [P, width], U32)
            z_sc = sb("z_sc%d" % i, [P, width], U8)
            for t in range(PACK):
                nc.scalar.activation(gate[t][:, :width], st[t][:].indirect(entries(n2_sb, start, width)), ACT.Sigmoid)
                nc.vector.scalar_tensor_tensor(
                    z_rows[:, t, :], sums1(t, start, width), gs16[:, t : t + 1], gate[t][:, :width], ALU.mult, ALU.mult
                )
            nc.vector.tensor_copy(
                z_words[:].rearrange("p (c i) t -> p c t i", i=4), z_rows[:].rearrange("p t (c i) -> p c t i", i=4)
            )
            nc.vector.quantize_mx(
                out=z_codes[:].bitcast(FP8X4), scales=z_sc[:], in_=z_words[:].rearrange("p c t -> p (c t)")
            )
            for t in range(PACK):
                product(acc2[i][t], t, z_codes[:], z_sc[:])

        y_words = [sb("y_words%d" % u, [P, S // 2, PACK], BF16) for u in range(2)]
        y_codes = sb("y_codes", [P, S], U32)
        y_sc = sb("y_sc", [P, S], U8)
        out_rows = out_0.rearrange("(p t) c -> t p c", t=PACK)
        old = [sb("old%d" % t, [P, W], F32) for t in range(PACK)]
        neg_tanh = [sb("neg_tanh%d" % t, [P, S], F32) for t in range(PACK)]
        ra = [sb("ra%d" % t, [P, W], F32) for t in range(PACK)]
        y = [sb("y%d" % t, [P, S], F32) for t in range(PACK)]

        def cols_of(i):
            start, width = PIECES[i]
            return slice(start, start + width)

        last = len(PIECES) - 1
        for i in range(last):
            nc.scalar.activation(h2[0][:, cols_of(i)], acc2[i][0], ACT.Copy, scale=SIXTEENTH)
            for t in range(PACK):
                nc.scalar.activation(neg_tanh[t][:, cols_of(i)], acc2[i][t], ACT.Tanh, scale=-SIXTEENTH)

        nc.scalar.activation(h2[0][:, cols_of(last)], acc2[last][0], ACT.Copy, scale=SIXTEENTH)
        for t in range(1, PACK):
            for i in range(len(PIECES)):
                nc.vector.tensor_scalar(h2[t][:, cols_of(i)], acc2[i][t], SIXTEENTH, None, ALU.mult)
        for t in range(PACK):
            nc.scalar.activation(old[t][:], h2[t][:].indirect(n3_sb[:]), ACT.Copy)
            nc.scalar.activation(neg_tanh[t][:, cols_of(last)], acc2[last][t], ACT.Tanh, scale=-SIXTEENTH)
        for t in range(PACK):
            nc.vector.tensor_copy(y[t][:], h2[t][:])
            nc.vector.tensor_tensor(ra[t][:], neg_tanh[t][:].indirect(n4_sb[:]), old[t][:], ALU.add)

        def put(t):
            nc.scalar.activation(y[t][:].indirect(n3_sb[:]), ra[t][:], ACT.Copy)
            nc.sync.dma_start(out_rows[t], y[t][:])
            for u in range(2):
                nc.vector.tensor_copy(y_words[u][:, :, t], y[t][:, u * S // 2 : (u + 1) * S // 2])

        for t in range(PACK):
            put(t)

        out_words = out_1[0].rearrange("p n t -> p (n t)").bitcast(I32)
        for u in range(2):
            cols = slice(u * S // 2, (u + 1) * S // 2)
            nc.vector.quantize_mx(
                out=y_codes[:, cols].bitcast(FP8X4), scales=y_sc[:, cols], in_=y_words[u][:].rearrange("p c t -> p (c t)")
            )
            nc.sync.dma_start(out_words[:, cols], y_codes[:, cols].bitcast(I32))
        for q in range(4):
            queue = nc.scalar if q % 2 == 0 else nc.sync
            queue.dma_start(out_2[0, 4 * q : 4 * q + 4, :].bitcast(I32), y_sc[32 * q : 32 * q + 4, :].bitcast(I32))
